import numpy as np
import ml_dtypes


def mxq(x, axis, fmt="e4m3"):
    dtype, down = {"e4m3": (ml_dtypes.float8_e4m3fn, 7), "e5m2": (ml_dtypes.float8_e5m2, 14)}[fmt]
    v = np.moveaxis(np.asarray(x, np.float32).astype(ml_dtypes.bfloat16).astype(np.float64), axis, -1)
    blocks = v.reshape(v.shape[:-1] + (-1, 32))
    amax = np.abs(blocks).max(-1, keepdims=True)
    byte = np.maximum(np.where(amax > 0, np.frexp(amax)[1] - 1 + 127, 0) - down, 1)
    scale = np.exp2(byte - 127.0)
    codes = (blocks / scale).astype(np.float32).astype(dtype).astype(np.float64)
    return np.moveaxis((codes * scale).reshape(v.shape), -1, axis)


WIDE = False


def mx_kscale(k):
    if not WIDE:
        return np.ones(k)
    levels = np.array([10, -10, 5, -5, 0])
    if k % 512:
        return np.exp2(np.random.permutation(np.resize(levels, k // 32))).repeat(32)
    a = np.empty((k // 512, 16))
    for p in range(k // 512):
        a[p, :8] = np.random.permutation(np.resize(levels, 8))
        for g in range(8):
            far = levels[np.abs(levels - a[p, g]) >= 10]
            a[p, g + 8] = far[np.random.randint(len(far))]
    return np.exp2(a.ravel()).repeat(32)


def f64(x):
    return np.asarray(x).astype(np.float64)


def striped(idx):
    return np.tile(idx.reshape(-1, 16).T, (8, 1)).astype(np.uint16)


def unstriped(offs):
    return offs[:16].T.reshape(-1).astype(np.int64)


def pack_weight(w):
    k, n = w.shape
    w = f64(np.asarray(w, np.float32).astype(ml_dtypes.bfloat16)).reshape(k // 32, 32, n)
    amax = np.abs(w).max(1)
    byte = np.clip(np.where(amax > 0, np.frexp(amax)[1] - 1 + 127 - 7, 1), 1, 254)
    scaled = (w * np.exp2(127.0 - byte)[:, None, :]).reshape(k, n).astype(np.float32)
    words = np.ascontiguousarray(scaled.reshape(k // 512, 128, 4, n).transpose(0, 1, 3, 2)).astype(ml_dtypes.float8_e4m3fn).view(np.uint8)
    return words, np.ascontiguousarray(byte.astype(np.uint8).reshape(k // 512, 16, n))


def unpack_weight(words, scales):
    g, p, n, _ = words.shape
    vals = np.ascontiguousarray(words).view(ml_dtypes.float8_e4m3fn).astype(np.float64) * np.repeat(np.exp2(scales.astype(np.float64) - 127.0), 8, axis=1)[..., None]
    return vals.transpose(0, 1, 3, 2).reshape(g * 512, n)


def gelu(v):
    return 0.5 * v * (1.0 + np.tanh(np.sqrt(2.0 / np.pi) * (v + 0.044715 * v**3)))


K, T, N = 512, 1024, 256
P = 2 ** 7


def setup_inputs():
    n = np.random.standard_normal
    s = mx_kscale(K)[:, None]
    packed_xT = pack_weight(n((K, T)) * s)
    return {
        "x_words": packed_xT[0],
        "x_scales": packed_xT[1],
        "w1": (n((K, N)) / np.sqrt(K) / s).astype(np.float32),
        "frac": np.tile(np.random.uniform(0.05, 0.95, T), (P, 1)).astype(np.float32),
        "left": striped(np.random.permutation(T)),
        "right": striped(np.random.permutation(T)),
    }


def reference(x_words, x_scales, w1, frac, left, right):
    xq = unpack_weight(x_words, x_scales)
    y = gelu(mxq(f64(w1), 0, "e4m3").T @ xq)
    l = y[:, unstriped(left)]
    return l + (y[:, unstriped(right)] - l) * f64(frac)[:1]

@@ -1,0 +1,103 @@
+from contextlib import ExitStack
+
+import concourse.mybir as mybir
+
+K, T, N = 512, 1024, 256
+FLOPS = 2 * K * T * N
+
+F32 = mybir.dt.float32
+BF16 = mybir.dt.bfloat16
+I32 = mybir.dt.int32
+U32 = mybir.dt.uint32
+U16 = mybir.dt.uint16
+U8 = mybir.dt.uint8
+FP8X4 = mybir.dt.float8_e4m3fn_x4
+MULT = mybir.AluOpType.mult
+ADD = mybir.AluOpType.add
+GELU = mybir.ActivationFunctionType.Gelu_apprx_tanh
+COPY = mybir.ActivationFunctionType.Copy
+
+P = 128
+PACK = 4
+HALF = 512
+
+
+def tile_picked_wlerp_gelu_l_kernel(tc, x_words, x_scales, w1, frac, left, right, out):
+    nc = tc.nc
+    with ExitStack() as ctx:
+        keep = ctx.enter_context(tc.tile_pool(name="keep", bufs=1))
+        psum = ctx.enter_context(tc.psum_pool(name="psum", bufs=1))
+
+        warm = keep.tile([P, 8], F32, name="warm")
+        warm_out = keep.tile([P, 8], F32, name="warm_out")
+        x_plane = keep.tile([P, T], U8, name="x_plane", align_bytes=64)
+        nc.vector.memset(x_plane[:].bitcast(I32), 0)
+        nc.vector.memset(warm[:], 0.0)
+        nc.scalar.activation(warm_out[:], warm[:], GELU)
+
+        w_view = w1.rearrange("(p j) n -> p j n", j=PACK)
+        w_raw = [keep.tile([P, PACK, P], F32, name="w_raw%d" % b) for b in range(2)]
+        x_codes = [keep.tile([P, HALF], U32, name="x_codes%d" % h, align_bytes=64) for h in range(2)]
+        x_flat = x_words[0].rearrange("p n t -> p (n t)")
+        left_sb = keep.tile([P, T // 16], U16, name="left_sb")
+        right_sb = keep.tile([P, T // 16], U16, name="right_sb")
+        f_sb = [keep.tile([P, HALF], F32, name="f_sb%d" % h) for h in range(2)]
+        g_sb = [keep.tile([P, HALF], F32, name="g_sb%d" % h) for h in range(2)]
+
+        nc.sync.dma_start(w_raw[0][:], w_view[:, :, 0:P])
+        for q in range(4):
+            nc.sync.dma_start(x_plane[32 * q : 32 * q + 4, :].bitcast(I32), x_scales[0, 4 * q : 4 * q + 4, :].bitcast(I32))
+        for h in range(2):
+            nc.sync.dma_start(x_codes[h][:].bitcast(I32), x_flat[:, h * HALF * PACK : (h + 1) * HALF * PACK].bitcast(I32))
+        nc.sync.dma_start(w_raw[1][:], w_view[:, :, P : 2 * P])
+        nc.sync.dma_start(right_sb[:], right)
+        nc.sync.dma_start(f_sb[0][:], frac[:, 0:HALF])
+        nc.sync.dma_start(left_sb[:], left)
+        nc.sync.dma_start(f_sb[1][:], frac[:, HALF:T])
+
+        y = []
+        for b in range(2):
+            w_bf = keep.tile([P, P, PACK], BF16, name="w_bf%d" % b, align_bytes=64)
+            w_codes = keep.tile([P, P], U32, name="w_codes%d" % b, align_bytes=64)
+            w_plane = keep.tile([P, P], U8, name="w_plane%d" % b, align_bytes=64)
+            nc.vector.tensor_copy(
+                w_bf[:].rearrange("p (c i) t -> p c t i", i=4), w_raw[b][:].rearrange("p t (c i) -> p c t i", i=4)
+            )
+            nc.vector.quantize_mx(out=w_codes[:].bitcast(FP8X4), scales=w_plane[:], in_=w_bf[:].rearrange("p n t -> p (n t)"))
+            y_b = keep.tile([P, T], F32, name="y%d" % b)
+            for h in range(2):
+                acc = psum.tile([P, HALF], F32, name="acc%d%d" % (b, h))
+                nc.tensor.matmul_mx(
+                    out=acc[:],
+                    lhsT=w_codes[:].bitcast(FP8X4),
+                    lhsT_scale=w_plane[:],
+                    rhs=x_codes[h][:].bitcast(FP8X4),
+                    rhs_scale=x_plane[:, h * HALF : (h + 1) * HALF],
+                    start=True,
+                    stop=True,
+                )
+                nc.scalar.activation(y_b[:, h * HALF : (h + 1) * HALF], acc[:], GELU)
+            y.append(y_b)
+            if b == 0:
+                for h in range(2):
+                    nc.scalar.activation(g_sb[h][:], f_sb[h][:], COPY, bias=1.0, scale=-1.0)
+
+        pieces = [(0, 0, 512), (0, 512, 512), (1, 0, 512), (1, 512, 256), (1, 768, 256)]
+        pending = None
+
+        def finish(b, v0, n, r_part, l_part):
+            res = keep.tile([P, n], F32, name="res%d_%d" % (b, v0))
+            nc.vector.tensor_tensor(res[:], r_part[:], l_part[:], ADD)
+            nc.sync.dma_start(out[b * P : (b + 1) * P, v0 : v0 + n], res[:])
+
+        for b, v0, n in pieces:
+            h, c0 = divmod(v0, HALF)
+            r_part = keep.tile([P, n], F32, name="r%d_%d" % (b, v0))
+            l_part = keep.tile([P, n], F32, name="l%d_%d" % (b, v0))
+            cols = slice(v0 // 16, (v0 + n) // 16)
+            nc.vector.tensor_tensor(r_part[:], y[b][:].indirect(right_sb[:, cols]), f_sb[h][:, c0 : c0 + n], MULT)
+            if pending is not None:
+                finish(*pending)
+            nc.vector.tensor_tensor(l_part[:], y[b][:].indirect(left_sb[:, cols]), g_sb[h][:, c0 : c0 + n], MULT)
+            pending = (b, v0, n, r_part, l_part)
+        finish(*pending)

@@ -1,6 +1,7 @@
 from contextlib import ExitStack
 
 import concourse.mybir as mybir
+from concourse.masks import make_identity
 
 K, T, N = 512, 1024, 256
 FLOPS = 2 * K * T * N
@@ -20,6 +21,9 @@ COPY = mybir.ActivationFunctionType.Copy
 P = 128
 PACK = 4
 HALF = 512
+X_CHUNKS = [(0, 512), (512, 512)]
+MM_CHUNKS = [[(0, 0, 256), (0, 256, 256), (1, 512, 256), (1, 768, 256)], [(0, 0, 512), (1, 512, 512)]]
+PIECES = [(0, 0, 256, True), (0, 256, 384, True), (0, 640, 384, True), (1, 0, 384, True), (1, 384, 256, True), (1, 640, 256, False), (1, 896, 128, False)]
 
 
 def tile_picked_wlerp_gelu_l_kernel(tc, x_words, x_scales, w1, frac, left, right, out):
@@ -27,77 +31,105 @@ def tile_picked_wlerp_gelu_l_kernel(tc, x_words, x_scales, w1, frac, left, right
     with ExitStack() as ctx:
         keep = ctx.enter_context(tc.tile_pool(name="keep", bufs=1))
         psum = ctx.enter_context(tc.psum_pool(name="psum", bufs=1))
+        turn = ctx.enter_context(tc.psum_pool(name="turn", bufs=2))
 
         warm = keep.tile([P, 8], F32, name="warm")
         warm_out = keep.tile([P, 8], F32, name="warm_out")
         x_plane = keep.tile([P, T], U8, name="x_plane", align_bytes=64)
-        nc.vector.memset(x_plane[:].bitcast(I32), 0)
+        ident = keep.tile([P, P], F32, name="ident")
+        nc.gpsimd.memset(x_plane[:].bitcast(I32), 0)
         nc.vector.memset(warm[:], 0.0)
-        nc.scalar.activation(warm_out[:], warm[:], GELU)
+        make_identity(nc, ident[:])
 
         w_view = w1.rearrange("(p j) n -> p j n", j=PACK)
         w_raw = [keep.tile([P, PACK, P], F32, name="w_raw%d" % b) for b in range(2)]
-        x_codes = [keep.tile([P, HALF], U32, name="x_codes%d" % h, align_bytes=64) for h in range(2)]
+        x_codes = [keep.tile([P, n], U32, name="x_codes%d" % c0, align_bytes=64) for c0, n in X_CHUNKS]
         x_flat = x_words[0].rearrange("p n t -> p (n t)")
         left_sb = keep.tile([P, T // 16], U16, name="left_sb")
         right_sb = keep.tile([P, T // 16], U16, name="right_sb")
-        f_sb = [keep.tile([P, HALF], F32, name="f_sb%d" % h) for h in range(2)]
-        g_sb = [keep.tile([P, HALF], F32, name="g_sb%d" % h) for h in range(2)]
+        f_sb = keep.tile([P, T], F32, name="f_sb")
+        g_sb = keep.tile([P, T], F32, name="g_sb")
 
-        nc.sync.dma_start(w_raw[0][:], w_view[:, :, 0:P])
-        for q in range(4):
-            nc.sync.dma_start(x_plane[32 * q : 32 * q + 4, :].bitcast(I32), x_scales[0, 4 * q : 4 * q + 4, :].bitcast(I32))
-        for h in range(2):
-            nc.sync.dma_start(x_codes[h][:].bitcast(I32), x_flat[:, h * HALF * PACK : (h + 1) * HALF * PACK].bitcast(I32))
-        nc.sync.dma_start(w_raw[1][:], w_view[:, :, P : 2 * P])
+        def ld_w(b):
+            nc.sync.dma_start(w_raw[b][:], w_view[:, :, b * P : (b + 1) * P])
+
+        def ld_s(q, eng):
+            eng.dma_start(x_plane[32 * q : 32 * q + 4, :].bitcast(I32), x_scales[0, 4 * q : 4 * q + 4, :].bitcast(I32))
+
+        def ld_x(i):
+            c0, n = X_CHUNKS[i]
+            nc.sync.dma_start(x_codes[i][:].bitcast(I32), x_flat[:, c0 * PACK : (c0 + n) * PACK].bitcast(I32))
+
+        def ld_f(c0, c1):
+            nc.sync.dma_start(f_sb[:, c0:c1], frac[:, c0:c1])
+
+        nc.scalar.activation(warm_out[:], warm[:], GELU)
         nc.sync.dma_start(right_sb[:], right)
-        nc.sync.dma_start(f_sb[0][:], frac[:, 0:HALF])
+        ld_w(0)
+        ld_x(0)
+        for q in range(4):
+            ld_s(q, nc.sync)
+        ld_x(1)
+        ld_f(0, 256)
         nc.sync.dma_start(left_sb[:], left)
-        nc.sync.dma_start(f_sb[1][:], frac[:, HALF:T])
+        ld_f(256, 640)
+        ld_w(1)
+        ld_f(640, T)
 
         y = []
         for b in range(2):
-            w_bf = keep.tile([P, P, PACK], BF16, name="w_bf%d" % b, align_bytes=64)
+            w_bf = keep.tile([P, P, PACK], BF16, name="w_bf%d" % b, tag="w_bf%d" % b, align_bytes=64)
             w_codes = keep.tile([P, P], U32, name="w_codes%d" % b, align_bytes=64)
             w_plane = keep.tile([P, P], U8, name="w_plane%d" % b, align_bytes=64)
-            nc.vector.tensor_copy(
-                w_bf[:].rearrange("p (c i) t -> p c t i", i=4), w_raw[b][:].rearrange("p t (c i) -> p c t i", i=4)
-            )
+            cast = nc.vector.tensor_copy if b == 0 else nc.scalar.copy
+            cast(w_bf[:].rearrange("p (c i) t -> p c t i", i=4), w_raw[b][:].rearrange("p t (c i) -> p c t i", i=4))
             nc.vector.quantize_mx(out=w_codes[:].bitcast(FP8X4), scales=w_plane[:], in_=w_bf[:].rearrange("p n t -> p (n t)"))
             y_b = keep.tile([P, T], F32, name="y%d" % b)
-            for h in range(2):
-                acc = psum.tile([P, HALF], F32, name="acc%d%d" % (b, h))
+            for i, (xi, c0, n) in enumerate(MM_CHUNKS[b]):
+                acc = psum.tile([P, n], F32, name="acc", tag="acc%d" % ((i + 2 * b) % 4))
+                x0 = c0 - X_CHUNKS[xi][0]
                 nc.tensor.matmul_mx(
                     out=acc[:],
                     lhsT=w_codes[:].bitcast(FP8X4),
                     lhsT_scale=w_plane[:],
-                    rhs=x_codes[h][:].bitcast(FP8X4),
-                    rhs_scale=x_plane[:, h * HALF : (h + 1) * HALF],
+                    rhs=x_codes[xi][:, x0 : x0 + n].bitcast(FP8X4),
+                    rhs_scale=x_plane[:, c0 : c0 + n],
                     start=True,
                     stop=True,
                 )
-                nc.scalar.activation(y_b[:, h * HALF : (h + 1) * HALF], acc[:], GELU)
+                nc.scalar.activation(y_b[:, c0 : c0 + n], acc[:], GELU)
             y.append(y_b)
             if b == 0:
-                for h in range(2):
-                    nc.scalar.activation(g_sb[h][:], f_sb[h][:], COPY, bias=1.0, scale=-1.0)
+                for c0, c1 in ((0, 256), (256, 640), (640, T)):
+                    nc.scalar.activation(g_sb[:, c0:c1], f_sb[:, c0:c1], COPY, bias=1.0, scale=-1.0)
 
-        pieces = [(0, 0, 512), (0, 512, 512), (1, 0, 512), (1, 512, 256), (1, 768, 256)]
-        pending = None
-
-        def finish(b, v0, n, r_part, l_part):
+        def finish(b, v0, n, on_tensor, r_part, l_part):
             res = keep.tile([P, n], F32, name="res%d_%d" % (b, v0))
-            nc.vector.tensor_tensor(res[:], r_part[:], l_part[:], ADD)
+            if on_tensor:
+                total = turn.tile([P, n], F32, name="total")
+                for j in range(0, n, P):
+                    blk = slice(j, j + P)
+                    nc.tensor.matmul(total[:, blk], r_part[:, blk], ident[:], start=True, stop=False, is_transpose=True)
+                    nc.tensor.matmul(total[:, blk], l_part[:, blk], ident[:], start=False, stop=True, is_transpose=True)
+                turned = keep.tile([P, n], F32, name="turned%d_%d" % (b, v0))
+                nc.scalar.copy(turned[:], total[:])
+                back = turn.tile([P, n], F32, name="back")
+                for j in range(0, n, P):
+                    blk = slice(j, j + P)
+                    nc.tensor.transpose(back[:, blk], turned[:, blk], ident[:])
+                nc.scalar.copy(res[:], back[:])
+            else:
+                nc.vector.tensor_tensor(res[:], r_part[:], l_part[:], ADD)
             nc.sync.dma_start(out[b * P : (b + 1) * P, v0 : v0 + n], res[:])
 
-        for b, v0, n in pieces:
-            h, c0 = divmod(v0, HALF)
+        pending = None
+        for b, v0, n, on_tensor in PIECES:
             r_part = keep.tile([P, n], F32, name="r%d_%d" % (b, v0))
-            l_part = keep.tile([P, n], F32, name="l%d_%d" % (b, v0))
+            l_part = keep.tile([P, n], F32, name="l%d_%d" % (b, v0), tag="w_bf1" if (b, v0) == (0, 256) else "l%d_%d" % (b, v0), align_bytes=64)
             cols = slice(v0 // 16, (v0 + n) // 16)
-            nc.vector.tensor_tensor(r_part[:], y[b][:].indirect(right_sb[:, cols]), f_sb[h][:, c0 : c0 + n], MULT)
+            nc.vector.tensor_tensor(r_part[:], y[b][:].indirect(right_sb[:, cols]), f_sb[:, v0 : v0 + n], MULT)
             if pending is not None:
                 finish(*pending)
-            nc.vector.tensor_tensor(l_part[:], y[b][:].indirect(left_sb[:, cols]), g_sb[h][:, c0 : c0 + n], MULT)
-            pending = (b, v0, n, r_part, l_part)
+            nc.vector.tensor_tensor(l_part[:], y[b][:].indirect(left_sb[:, cols]), g_sb[:, v0 : v0 + n], MULT)
+            pending = (b, v0, n, on_tensor, r_part, l_part)
         finish(*pending)

@@ -22,8 +22,9 @@ P = 128
 PACK = 4
 HALF = 512
 X_CHUNKS = [(0, 512), (512, 512)]
-MM_CHUNKS = [[(0, 0, 256), (0, 256, 256), (1, 512, 256), (1, 768, 256)], [(0, 0, 512), (1, 512, 512)]]
-PIECES = [(0, 0, 256, True), (0, 256, 384, True), (0, 640, 384, True), (1, 0, 384, True), (1, 384, 256, True), (1, 640, 256, False), (1, 896, 128, False)]
+MM_CHUNKS = [[(0, 0, 128), (0, 128, 128), (0, 256, 256), (1, 512, 256), (1, 768, 128), (1, 896, 128)], [(0, 0, 512), (1, 512, 512)]]
+PIECES = [("r", 0, 0, 384), ("l", 0, 0, 384), ("t", 0, 0, 256), ("t", 0, 256, 128), ("r", 0, 384, 640), ("l", 0, 384, 640), ("t", 0, 384, 256), ("t", 0, 640, 256), ("t", 0, 896, 128),
+    ("r", 1, 0, 384), ("l", 1, 0, 384), ("t", 1, 0, 256), ("t", 1, 256, 128), ("r", 1, 384, 512), ("l", 1, 384, 512), ("r", 1, 896, 128), ("v", 1, 384, 512), ("l", 1, 896, 128), ("v", 1, 896, 128)]
 
 
 def tile_picked_wlerp_gelu_l_kernel(tc, x_words, x_scales, w1, frac, left, right, out):
@@ -70,11 +71,10 @@ def tile_picked_wlerp_gelu_l_kernel(tc, x_words, x_scales, w1, frac, left, right
         for q in range(4):
             ld_s(q, nc.sync)
         ld_x(1)
-        ld_f(0, 256)
+        ld_f(0, 384)
         nc.sync.dma_start(left_sb[:], left)
-        ld_f(256, 640)
         ld_w(1)
-        ld_f(640, T)
+        ld_f(384, T)
 
         y = []
         for b in range(2):
@@ -82,8 +82,11 @@ def tile_picked_wlerp_gelu_l_kernel(tc, x_words, x_scales, w1, frac, left, right
             w_codes = keep.tile([P, P], U32, name="w_codes%d" % b, align_bytes=64)
             w_plane = keep.tile([P, P], U8, name="w_plane%d" % b, align_bytes=64)
             cast = nc.vector.tensor_copy if b == 0 else nc.scalar.copy
-            cast(w_bf[:].rearrange("p (c i) t -> p c t i", i=4), w_raw[b][:].rearrange("p t (c i) -> p c t i", i=4))
-            nc.vector.quantize_mx(out=w_codes[:].bitcast(FP8X4), scales=w_plane[:], in_=w_bf[:].rearrange("p n t -> p (n t)"))
+            spans = [slice(0, 64), slice(64, P)] if b == 0 else [slice(0, P)]
+            for s in spans:
+                cast(w_bf[:, s, :].rearrange("p (c i) t -> p c t i", i=4), w_raw[b][:, :, s].rearrange("p t (c i) -> p c t i", i=4))
+            for s in spans:
+                nc.vector.quantize_mx(out=w_codes[:, s].bitcast(FP8X4), scales=w_plane[:, s], in_=w_bf[:, s, :].rearrange("p n t -> p (n t)"))
             y_b = keep.tile([P, T], F32, name="y%d" % b)
             for i, (xi, c0, n) in enumerate(MM_CHUNKS[b]):
                 acc = psum.tile([P, n], F32, name="acc", tag="acc%d" % ((i + 2 * b) % 4))
@@ -100,17 +103,25 @@ def tile_picked_wlerp_gelu_l_kernel(tc, x_words, x_scales, w1, frac, left, right
                 nc.scalar.activation(y_b[:, c0 : c0 + n], acc[:], GELU)
             y.append(y_b)
             if b == 0:
-                for c0, c1 in ((0, 256), (256, 640), (640, T)):
+                for c0, c1 in ((0, 384), (384, T)):
                     nc.scalar.activation(g_sb[:, c0:c1], f_sb[:, c0:c1], COPY, bias=1.0, scale=-1.0)
 
-        def finish(b, v0, n, on_tensor, r_part, l_part):
+        parts = {"r": [], "l": []}
+
+        def part(kind, b, v0, n):
+            for pb, p0, pn, tile in parts[kind]:
+                if pb == b and p0 <= v0 and v0 + n <= p0 + pn:
+                    return tile[:, v0 - p0 : v0 - p0 + n]
+            raise ValueError("no such part")
+
+        def finish(b, v0, n, on_tensor):
             res = keep.tile([P, n], F32, name="res%d_%d" % (b, v0))
             if on_tensor:
                 total = turn.tile([P, n], F32, name="total")
                 for j in range(0, n, P):
                     blk = slice(j, j + P)
-                    nc.tensor.matmul(total[:, blk], r_part[:, blk], ident[:], start=True, stop=False, is_transpose=True)
-                    nc.tensor.matmul(total[:, blk], l_part[:, blk], ident[:], start=False, stop=True, is_transpose=True)
+                    nc.tensor.matmul(total[:, blk], part("r", b, v0 + j, P), ident[:], start=True, stop=False, is_transpose=True)
+                    nc.tensor.matmul(total[:, blk], part("l", b, v0 + j, P), ident[:], start=False, stop=True, is_transpose=True)
                 turned = keep.tile([P, n], F32, name="turned%d_%d" % (b, v0))
                 nc.scalar.copy(turned[:], total[:])
                 back = turn.tile([P, n], F32, name="back")
@@ -119,17 +130,15 @@ def tile_picked_wlerp_gelu_l_kernel(tc, x_words, x_scales, w1, frac, left, right
                     nc.tensor.transpose(back[:, blk], turned[:, blk], ident[:])
                 nc.scalar.copy(res[:], back[:])
             else:
-                nc.vector.tensor_tensor(res[:], r_part[:], l_part[:], ADD)
+                nc.vector.tensor_tensor(res[:], part("r", b, v0, n), part("l", b, v0, n), ADD)
             nc.sync.dma_start(out[b * P : (b + 1) * P, v0 : v0 + n], res[:])
 
-        pending = None
-        for b, v0, n, on_tensor in PIECES:
-            r_part = keep.tile([P, n], F32, name="r%d_%d" % (b, v0))
-            l_part = keep.tile([P, n], F32, name="l%d_%d" % (b, v0), tag="w_bf1" if (b, v0) == (0, 256) else "l%d_%d" % (b, v0), align_bytes=64)
-            cols = slice(v0 // 16, (v0 + n) // 16)
-            nc.vector.tensor_tensor(r_part[:], y[b][:].indirect(right_sb[:, cols]), f_sb[:, v0 : v0 + n], MULT)
-            if pending is not None:
-                finish(*pending)
-            nc.vector.tensor_tensor(l_part[:], y[b][:].indirect(left_sb[:, cols]), g_sb[:, v0 : v0 + n], MULT)
-            pending = (b, v0, n, on_tensor, r_part, l_part)
-        finish(*pending)
+        for kind, b, v0, n in PIECES:
+            if kind in parts:
+                name = "%s%d_%d" % (kind, b, v0)
+                got = keep.tile([P, n], F32, name=name, tag="w_bf1" if (kind, b, v0) == ("r", 0, 384) else name, align_bytes=64)
+                offsets, factor = (right_sb, f_sb) if kind == "r" else (left_sb, g_sb)
+                nc.vector.tensor_tensor(got[:], y[b][:].indirect(offsets[:, v0 // 16 : (v0 + n) // 16]), factor[:, v0 : v0 + n], MULT)
+                parts[kind].append((b, v0, n, got))
+            else:
+                finish(b, v0, n, kind == "t")

@@ -20,125 +20,139 @@ COPY = mybir.ActivationFunctionType.Copy
 
 P = 128
 PACK = 4
-HALF = 512
-X_CHUNKS = [(0, 512), (512, 512)]
-MM_CHUNKS = [[(0, 0, 128), (0, 128, 128), (0, 256, 256), (1, 512, 256), (1, 768, 128), (1, 896, 128)], [(0, 0, 512), (1, 512, 512)]]
-PIECES = [("r", 0, 0, 384), ("l", 0, 0, 384), ("t", 0, 0, 256), ("t", 0, 256, 128), ("r", 0, 384, 640), ("l", 0, 384, 640), ("t", 0, 384, 256), ("t", 0, 640, 256), ("t", 0, 896, 128),
-    ("r", 1, 0, 384), ("l", 1, 0, 384), ("t", 1, 0, 256), ("t", 1, 256, 128), ("r", 1, 384, 512), ("l", 1, 384, 512), ("r", 1, 896, 128), ("v", 1, 384, 512), ("l", 1, 896, 128), ("v", 1, 896, 128)]
+GROUP = 16
+HALF = T // 2
+PRODUCT_BANKS = 4
+
+PRODUCT_WIDTHS = ((128, 128, 256, 256, 128, 128), (512, 512))
+
+SPLIT = 384
+LAST = 128
 
 
 def tile_picked_wlerp_gelu_l_kernel(tc, x_words, x_scales, w1, frac, left, right, out):
     nc = tc.nc
     with ExitStack() as ctx:
         keep = ctx.enter_context(tc.tile_pool(name="keep", bufs=1))
-        psum = ctx.enter_context(tc.psum_pool(name="psum", bufs=1))
-        turn = ctx.enter_context(tc.psum_pool(name="turn", bufs=2))
+        products = ctx.enter_context(tc.psum_pool(name="products", bufs=1))
+        turns = ctx.enter_context(tc.psum_pool(name="turns", bufs=2))
 
-        warm = keep.tile([P, 8], F32, name="warm")
-        warm_out = keep.tile([P, 8], F32, name="warm_out")
-        x_plane = keep.tile([P, T], U8, name="x_plane", align_bytes=64)
-        ident = keep.tile([P, P], F32, name="ident")
-        nc.gpsimd.memset(x_plane[:].bitcast(I32), 0)
-        nc.vector.memset(warm[:], 0.0)
-        make_identity(nc, ident[:])
+        x_scale = keep.tile([P, T], U8, name="x_scale", align_bytes=64)
+        identity = keep.tile([P, P], F32, name="identity")
+        nc.gpsimd.memset(x_scale[:].bitcast(I32), 0)
+        make_identity(nc, identity[:])
 
-        w_view = w1.rearrange("(p j) n -> p j n", j=PACK)
+        w_rows = w1.rearrange("(p j) n -> p j n", j=PACK)
+        x_bytes = x_words[0].rearrange("p n t -> p (n t)")
         w_raw = [keep.tile([P, PACK, P], F32, name="w_raw%d" % b) for b in range(2)]
-        x_codes = [keep.tile([P, n], U32, name="x_codes%d" % c0, align_bytes=64) for c0, n in X_CHUNKS]
-        x_flat = x_words[0].rearrange("p n t -> p (n t)")
-        left_sb = keep.tile([P, T // 16], U16, name="left_sb")
-        right_sb = keep.tile([P, T // 16], U16, name="right_sb")
-        f_sb = keep.tile([P, T], F32, name="f_sb")
-        g_sb = keep.tile([P, T], F32, name="g_sb")
+        x_codes = [keep.tile([P, HALF], U32, name="x_codes%d" % h, align_bytes=64) for h in range(2)]
+        left_list = keep.tile([P, T // GROUP], U16, name="left_list")
+        right_list = keep.tile([P, T // GROUP], U16, name="right_list")
+        right_factor = keep.tile([P, T], F32, name="right_factor")
+        left_factor = keep.tile([P, T], F32, name="left_factor")
 
-        def ld_w(b):
-            nc.sync.dma_start(w_raw[b][:], w_view[:, :, b * P : (b + 1) * P])
+        def load_w(b):
+            nc.sync.dma_start(w_raw[b][:], w_rows[:, :, b * P : (b + 1) * P])
 
-        def ld_s(q, eng):
-            eng.dma_start(x_plane[32 * q : 32 * q + 4, :].bitcast(I32), x_scales[0, 4 * q : 4 * q + 4, :].bitcast(I32))
+        def load_x(h):
+            nc.sync.dma_start(x_codes[h][:].bitcast(I32), x_bytes[:, h * HALF * PACK : (h + 1) * HALF * PACK].bitcast(I32))
 
-        def ld_x(i):
-            c0, n = X_CHUNKS[i]
-            nc.sync.dma_start(x_codes[i][:].bitcast(I32), x_flat[:, c0 * PACK : (c0 + n) * PACK].bitcast(I32))
-
-        def ld_f(c0, c1):
-            nc.sync.dma_start(f_sb[:, c0:c1], frac[:, c0:c1])
-
-        nc.scalar.activation(warm_out[:], warm[:], GELU)
-        nc.sync.dma_start(right_sb[:], right)
-        ld_w(0)
-        ld_x(0)
+        nc.sync.dma_start(right_list[:], right)
+        load_w(0)
+        load_x(0)
         for q in range(4):
-            ld_s(q, nc.sync)
-        ld_x(1)
-        ld_f(0, 384)
-        nc.sync.dma_start(left_sb[:], left)
-        ld_w(1)
-        ld_f(384, T)
+            nc.sync.dma_start(x_scale[32 * q : 32 * q + 4, :].bitcast(I32), x_scales[0, 4 * q : 4 * q + 4, :].bitcast(I32))
+        load_x(1)
+        nc.sync.dma_start(right_factor[:, 0:SPLIT], frac[:, 0:SPLIT])
+        nc.sync.dma_start(left_list[:], left)
+        load_w(1)
+        nc.sync.dma_start(right_factor[:, SPLIT:T], frac[:, SPLIT:T])
 
-        y = []
-        for b in range(2):
-            w_bf = keep.tile([P, P, PACK], BF16, name="w_bf%d" % b, tag="w_bf%d" % b, align_bytes=64)
+        def project(b, cast, column_spans):
+            w_bf16 = keep.tile([P, P, PACK], BF16, name="w_bf16", tag="w_bf16_%d" % b, align_bytes=64)
             w_codes = keep.tile([P, P], U32, name="w_codes%d" % b, align_bytes=64)
-            w_plane = keep.tile([P, P], U8, name="w_plane%d" % b, align_bytes=64)
-            cast = nc.vector.tensor_copy if b == 0 else nc.scalar.copy
-            spans = [slice(0, 64), slice(64, P)] if b == 0 else [slice(0, P)]
-            for s in spans:
-                cast(w_bf[:, s, :].rearrange("p (c i) t -> p c t i", i=4), w_raw[b][:, :, s].rearrange("p t (c i) -> p c t i", i=4))
-            for s in spans:
-                nc.vector.quantize_mx(out=w_codes[:, s].bitcast(FP8X4), scales=w_plane[:, s], in_=w_bf[:, s, :].rearrange("p n t -> p (n t)"))
-            y_b = keep.tile([P, T], F32, name="y%d" % b)
-            for i, (xi, c0, n) in enumerate(MM_CHUNKS[b]):
-                acc = psum.tile([P, n], F32, name="acc", tag="acc%d" % ((i + 2 * b) % 4))
-                x0 = c0 - X_CHUNKS[xi][0]
+            w_scale = keep.tile([P, P], U8, name="w_scale%d" % b, align_bytes=64)
+            for span in column_spans:
+                cast(
+                    w_bf16[:, span, :].rearrange("p (c i) t -> p c t i", i=4),
+                    w_raw[b][:, :, span].rearrange("p t (c i) -> p c t i", i=4),
+                )
+            for span in column_spans:
+                nc.vector.quantize_mx(
+                    out=w_codes[:, span].bitcast(FP8X4),
+                    scales=w_scale[:, span],
+                    in_=w_bf16[:, span, :].rearrange("p n t -> p (n t)"),
+                )
+            y_tile = keep.tile([P, T], F32, name="y%d" % b)
+            start = 0
+            for i, width in enumerate(PRODUCT_WIDTHS[b]):
+                bank = (len(PRODUCT_WIDTHS[0]) * b + i) % PRODUCT_BANKS
+                product = products.tile([P, width], F32, name="product", tag="product%d" % bank)
+                h, inside = divmod(start, HALF)
                 nc.tensor.matmul_mx(
-                    out=acc[:],
+                    out=product[:],
                     lhsT=w_codes[:].bitcast(FP8X4),
-                    lhsT_scale=w_plane[:],
-                    rhs=x_codes[xi][:, x0 : x0 + n].bitcast(FP8X4),
-                    rhs_scale=x_plane[:, c0 : c0 + n],
+                    lhsT_scale=w_scale[:],
+                    rhs=x_codes[h][:, inside : inside + width].bitcast(FP8X4),
+                    rhs_scale=x_scale[:, start : start + width],
                     start=True,
                     stop=True,
                 )
-                nc.scalar.activation(y_b[:, c0 : c0 + n], acc[:], GELU)
-            y.append(y_b)
-            if b == 0:
-                for c0, c1 in ((0, 384), (384, T)):
-                    nc.scalar.activation(g_sb[:, c0:c1], f_sb[:, c0:c1], COPY, bias=1.0, scale=-1.0)
+                nc.scalar.activation(y_tile[:, start : start + width], product[:], GELU)
+                start += width
+            return y_tile
 
-        parts = {"r": [], "l": []}
+        y = [project(0, nc.vector.tensor_copy, (slice(0, P // 2), slice(P // 2, P)))]
+        nc.scalar.activation(left_factor[:, 0:SPLIT], right_factor[:, 0:SPLIT], COPY, bias=1.0, scale=-1.0)
+        y.append(project(1, nc.scalar.copy, (slice(0, P),)))
+        nc.scalar.activation(left_factor[:, SPLIT:T], right_factor[:, SPLIT:T], COPY, bias=1.0, scale=-1.0)
 
-        def part(kind, b, v0, n):
-            for pb, p0, pn, tile in parts[kind]:
-                if pb == b and p0 <= v0 and v0 + n <= p0 + pn:
-                    return tile[:, v0 - p0 : v0 - p0 + n]
-            raise ValueError("no such part")
+        def gather(b, offsets, factor, v0, v1, tag):
+            term = keep.tile([P, v1 - v0], F32, name="term", tag=tag, align_bytes=64)
+            window = y[b][:].indirect(offsets[:, v0 // GROUP : v1 // GROUP])
+            nc.vector.tensor_tensor(term[:], window, factor[:, v0:v1], MULT)
+            return term
 
-        def finish(b, v0, n, on_tensor):
-            res = keep.tile([P, n], F32, name="res%d_%d" % (b, v0))
-            if on_tensor:
-                total = turn.tile([P, n], F32, name="total")
-                for j in range(0, n, P):
-                    blk = slice(j, j + P)
-                    nc.tensor.matmul(total[:, blk], part("r", b, v0 + j, P), ident[:], start=True, stop=False, is_transpose=True)
-                    nc.tensor.matmul(total[:, blk], part("l", b, v0 + j, P), ident[:], start=False, stop=True, is_transpose=True)
-                turned = keep.tile([P, n], F32, name="turned%d_%d" % (b, v0))
-                nc.scalar.copy(turned[:], total[:])
-                back = turn.tile([P, n], F32, name="back")
-                for j in range(0, n, P):
-                    blk = slice(j, j + P)
-                    nc.tensor.transpose(back[:, blk], turned[:, blk], ident[:])
-                nc.scalar.copy(res[:], back[:])
-            else:
-                nc.vector.tensor_tensor(res[:], part("r", b, v0, n), part("l", b, v0, n), ADD)
-            nc.sync.dma_start(out[b * P : (b + 1) * P, v0 : v0 + n], res[:])
+        def sum_by_transposes(b, right_term, left_term, base, v0, v1, tag):
+            width = v1 - v0
+            turned_psum = turns.tile([P, width], F32, name="turned_psum")
+            for j in range(0, width, P):
+                source = slice(v0 - base + j, v0 - base + j + P)
+                for term, first in ((right_term, True), (left_term, False)):
+                    nc.tensor.matmul(
+                        turned_psum[:, j : j + P], term[:, source], identity[:], start=first, stop=not first, is_transpose=True
+                    )
+            turned = keep.tile([P, width], F32, name="turned", tag=tag)
+            nc.scalar.copy(turned[:], turned_psum[:])
+            result_psum = turns.tile([P, width], F32, name="result_psum")
+            for j in range(0, width, P):
+                nc.tensor.transpose(result_psum[:, j : j + P], turned[:, j : j + P], identity[:])
+            result = keep.tile([P, width], F32, name="result%d_%d" % (b, v0))
+            nc.scalar.copy(result[:], result_psum[:])
+            nc.sync.dma_start(out[b * P : (b + 1) * P, v0:v1], result[:])
 
-        for kind, b, v0, n in PIECES:
-            if kind in parts:
-                name = "%s%d_%d" % (kind, b, v0)
-                got = keep.tile([P, n], F32, name=name, tag="w_bf1" if (kind, b, v0) == ("r", 0, 384) else name, align_bytes=64)
-                offsets, factor = (right_sb, f_sb) if kind == "r" else (left_sb, g_sb)
-                nc.vector.tensor_tensor(got[:], y[b][:].indirect(offsets[:, v0 // 16 : (v0 + n) // 16]), factor[:, v0 : v0 + n], MULT)
-                parts[kind].append((b, v0, n, got))
-            else:
-                finish(b, v0, n, kind == "t")
+        right_term = gather(0, right_list, right_factor, 0, SPLIT, "right0a")
+        left_term = gather(0, left_list, left_factor, 0, SPLIT, "left0a")
+        sum_by_transposes(0, right_term, left_term, 0, 0, SPLIT, "turned0a")
+        right_term = gather(0, right_list, right_factor, SPLIT, T, "w_bf16_1")
+        left_term = gather(0, left_list, left_factor, SPLIT, T, "left0b")
+        sum_by_transposes(0, right_term, left_term, SPLIT, SPLIT, 2 * SPLIT, "turned0b")
+        sum_by_transposes(0, right_term, left_term, SPLIT, 2 * SPLIT, T, "turned0c")
+
+        right_term = gather(1, right_list, right_factor, 0, SPLIT, "right1a")
+        left_term = gather(1, left_list, left_factor, 0, SPLIT, "left1a")
+        sum_by_transposes(1, right_term, left_term, 0, 0, SPLIT - P, "turned1a")
+        sum_by_transposes(1, right_term, left_term, 0, SPLIT - P, SPLIT, "turned_last")
+
+        right_term = gather(1, right_list, right_factor, SPLIT, T, "right1b")
+        left_term = gather(1, left_list, left_factor, SPLIT, T - LAST, "left1b")
+        left_last = gather(1, left_list, left_factor, T - LAST, T, "left1c")
+        result = keep.tile([P, T - SPLIT], F32, name="result_tail", tag="turned_last")
+        wide = T - LAST - SPLIT
+        for c0, c1, left_part in (
+            (0, wide // 2, left_term[:, 0 : wide // 2]),
+            (wide // 2, wide, left_term[:, wide // 2 : wide]),
+            (wide, wide + LAST, left_last[:]),
+        ):
+            nc.vector.tensor_tensor(result[:, c0:c1], right_term[:, c0:c1], left_part, ADD)
+            nc.sync.dma_start(out[P : 2 * P, SPLIT + c0 : SPLIT + c1], result[:, c0:c1])

@@ -37,10 +37,14 @@ def tile_picked_wlerp_gelu_l_kernel(tc, x_words, x_scales, w1, frac, left, right
         products = ctx.enter_context(tc.psum_pool(name="products", bufs=1))
         turns = ctx.enter_context(tc.psum_pool(name="turns", bufs=2))
 
+        warm_in = keep.tile([P, 8], F32, name="warm_in")
+        warm_out = keep.tile([P, 8], F32, name="warm_out")
         x_scale = keep.tile([P, T], U8, name="x_scale", align_bytes=64)
         identity = keep.tile([P, P], F32, name="identity")
         nc.gpsimd.memset(x_scale[:].bitcast(I32), 0)
+        nc.vector.memset(warm_in[:], 0.0)
         make_identity(nc, identity[:])
+        nc.scalar.activation(warm_out[:], warm_in[:], GELU)
 
         w_rows = w1.rearrange("(p j) n -> p j n", j=PACK)
         x_bytes = x_words[0].rearrange("p n t -> p (n t)")

from contextlib import ExitStack

import concourse.mybir as mybir
from concourse.masks import make_identity

K, T, N = 512, 1024, 256
FLOPS = 2 * K * T * N

F32 = mybir.dt.float32
BF16 = mybir.dt.bfloat16
I32 = mybir.dt.int32
U32 = mybir.dt.uint32
U16 = mybir.dt.uint16
U8 = mybir.dt.uint8
FP8X4 = mybir.dt.float8_e4m3fn_x4
MULT = mybir.AluOpType.mult
ADD = mybir.AluOpType.add
GELU = mybir.ActivationFunctionType.Gelu_apprx_tanh
COPY = mybir.ActivationFunctionType.Copy

P = 128
PACK = 4
GROUP = 16
HALF = T // 2
PRODUCT_BANKS = 4

PRODUCT_WIDTHS = ((128, 128, 256, 256, 128, 128), (512, 512))

SPLIT = 384
LAST = 128


def tile_picked_wlerp_gelu_l_kernel(tc, x_words, x_scales, w1, frac, left, right, out):
    nc = tc.nc
    with ExitStack() as ctx:
        keep = ctx.enter_context(tc.tile_pool(name="keep", bufs=1))
        products = ctx.enter_context(tc.psum_pool(name="products", bufs=1))
        turns = ctx.enter_context(tc.psum_pool(name="turns", bufs=2))

        warm_in = keep.tile([P, 8], F32, name="warm_in")
        warm_out = keep.tile([P, 8], F32, name="warm_out")
        x_scale = keep.tile([P, T], U8, name="x_scale", align_bytes=64)
        identity = keep.tile([P, P], F32, name="identity")
        nc.gpsimd.memset(x_scale[:].bitcast(I32), 0)
        nc.vector.memset(warm_in[:], 0.0)
        make_identity(nc, identity[:])
        nc.scalar.activation(warm_out[:], warm_in[:], GELU)

        w_rows = w1.rearrange("(p j) n -> p j n", j=PACK)
        x_bytes = x_words[0].rearrange("p n t -> p (n t)")
        w_raw = [keep.tile([P, PACK, P], F32, name="w_raw%d" % b) for b in range(2)]
        x_codes = [keep.tile([P, HALF], U32, name="x_codes%d" % h, align_bytes=64) for h in range(2)]
        left_list = keep.tile([P, T // GROUP], U16, name="left_list")
        right_list = keep.tile([P, T // GROUP], U16, name="right_list")
        right_factor = keep.tile([P, T], F32, name="right_factor")
        left_factor = keep.tile([P, T], F32, name="left_factor")

        def load_w(b):
            nc.sync.dma_start(w_raw[b][:], w_rows[:, :, b * P : (b + 1) * P])

        def load_x(h):
            nc.sync.dma_start(x_codes[h][:].bitcast(I32), x_bytes[:, h * HALF * PACK : (h + 1) * HALF * PACK].bitcast(I32))

        nc.sync.dma_start(right_list[:], right)
        load_w(0)
        load_x(0)
        for q in range(4):
            nc.sync.dma_start(x_scale[32 * q : 32 * q + 4, :].bitcast(I32), x_scales[0, 4 * q : 4 * q + 4, :].bitcast(I32))
        load_x(1)
        nc.sync.dma_start(right_factor[:, 0:SPLIT], frac[:, 0:SPLIT])
        nc.sync.dma_start(left_list[:], left)
        load_w(1)
        nc.sync.dma_start(right_factor[:, SPLIT:T], frac[:, SPLIT:T])

        def project(b, cast, column_spans):
            w_bf16 = keep.tile([P, P, PACK], BF16, name="w_bf16", tag="w_bf16_%d" % b, align_bytes=64)
            w_codes = keep.tile([P, P], U32, name="w_codes%d" % b, align_bytes=64)
            w_scale = keep.tile([P, P], U8, name="w_scale%d" % b, align_bytes=64)
            for span in column_spans:
                cast(
                    w_bf16[:, span, :].rearrange("p (c i) t -> p c t i", i=4),
                    w_raw[b][:, :, span].rearrange("p t (c i) -> p c t i", i=4),
                )
            for span in column_spans:
                nc.vector.quantize_mx(
                    out=w_codes[:, span].bitcast(FP8X4),
                    scales=w_scale[:, span],
                    in_=w_bf16[:, span, :].rearrange("p n t -> p (n t)"),
                )
            y_tile = keep.tile([P, T], F32, name="y%d" % b)
            start = 0
            for i, width in enumerate(PRODUCT_WIDTHS[b]):
                bank = (len(PRODUCT_WIDTHS[0]) * b + i) % PRODUCT_BANKS
                product = products.tile([P, width], F32, name="product", tag="product%d" % bank)
                h, inside = divmod(start, HALF)
                nc.tensor.matmul_mx(
                    out=product[:],
                    lhsT=w_codes[:].bitcast(FP8X4),
                    lhsT_scale=w_scale[:],
                    rhs=x_codes[h][:, inside : inside + width].bitcast(FP8X4),
                    rhs_scale=x_scale[:, start : start + width],
                    start=True,
                    stop=True,
                )
                nc.scalar.activation(y_tile[:, start : start + width], product[:], GELU)
                start += width
            return y_tile

        y = [project(0, nc.vector.tensor_copy, (slice(0, P // 2), slice(P // 2, P)))]
        nc.scalar.activation(left_factor[:, 0:SPLIT], right_factor[:, 0:SPLIT], COPY, bias=1.0, scale=-1.0)
        y.append(project(1, nc.scalar.copy, (slice(0, P),)))
        nc.scalar.activation(left_factor[:, SPLIT:T], right_factor[:, SPLIT:T], COPY, bias=1.0, scale=-1.0)

        def gather(b, offsets, factor, v0, v1, tag):
            term = keep.tile([P, v1 - v0], F32, name="term", tag=tag, align_bytes=64)
            window = y[b][:].indirect(offsets[:, v0 // GROUP : v1 // GROUP])
            nc.vector.tensor_tensor(term[:], window, factor[:, v0:v1], MULT)
            return term

        def sum_by_transposes(b, right_term, left_term, base, v0, v1, tag):
            width = v1 - v0
            turned_psum = turns.tile([P, width], F32, name="turned_psum")
            for j in range(0, width, P):
                source = slice(v0 - base + j, v0 - base + j + P)
                for term, first in ((right_term, True), (left_term, False)):
                    nc.tensor.matmul(
                        turned_psum[:, j : j + P], term[:, source], identity[:], start=first, stop=not first, is_transpose=True
                    )
            turned = keep.tile([P, width], F32, name="turned", tag=tag)
            nc.scalar.copy(turned[:], turned_psum[:])
            result_psum = turns.tile([P, width], F32, name="result_psum")
            for j in range(0, width, P):
                nc.tensor.transpose(result_psum[:, j : j + P], turned[:, j : j + P], identity[:])
            result = keep.tile([P, width], F32, name="result%d_%d" % (b, v0))
            nc.scalar.copy(result[:], result_psum[:])
            nc.sync.dma_start(out[b * P : (b + 1) * P, v0:v1], result[:])

        right_term = gather(0, right_list, right_factor, 0, SPLIT, "right0a")
        left_term = gather(0, left_list, left_factor, 0, SPLIT, "left0a")
        sum_by_transposes(0, right_term, left_term, 0, 0, SPLIT, "turned0a")
        right_term = gather(0, right_list, right_factor, SPLIT, T, "w_bf16_1")
        left_term = gather(0, left_list, left_factor, SPLIT, T, "left0b")
        sum_by_transposes(0, right_term, left_term, SPLIT, SPLIT, 2 * SPLIT, "turned0b")
        sum_by_transposes(0, right_term, left_term, SPLIT, 2 * SPLIT, T, "turned0c")

        right_term = gather(1, right_list, right_factor, 0, SPLIT, "right1a")
        left_term = gather(1, left_list, left_factor, 0, SPLIT, "left1a")
        sum_by_transposes(1, right_term, left_term, 0, 0, SPLIT - P, "turned1a")
        sum_by_transposes(1, right_term, left_term, 0, SPLIT - P, SPLIT, "turned_last")

        right_term = gather(1, right_list, right_factor, SPLIT, T, "right1b")
        left_term = gather(1, left_list, left_factor, SPLIT, T - LAST, "left1b")
        left_last = gather(1, left_list, left_factor, T - LAST, T, "left1c")
        result = keep.tile([P, T - SPLIT], F32, name="result_tail", tag="turned_last")
        wide = T - LAST - SPLIT
        for c0, c1, left_part in (
            (0, wide // 2, left_term[:, 0 : wide // 2]),
            (wide // 2, wide, left_term[:, wide // 2 : wide]),
            (wide, wide + LAST, left_last[:]),
        ):
            nc.vector.tensor_tensor(result[:, c0:c1], right_term[:, c0:c1], left_part, ADD)
            nc.sync.dma_start(out[P : 2 * P, SPLIT + c0 : SPLIT + c1], result[:, c0:c1])
